import numpy as np
import ml_dtypes


def mxq(x, axis, fmt="e4m3"):
    dtype, down = {"e4m3": (ml_dtypes.float8_e4m3fn, 7), "e5m2": (ml_dtypes.float8_e5m2, 14)}[fmt]
    v = np.moveaxis(np.asarray(x, np.float32).astype(ml_dtypes.bfloat16).astype(np.float64), axis, -1)
    blocks = v.reshape(v.shape[:-1] + (-1, 32))
    amax = np.abs(blocks).max(-1, keepdims=True)
    byte = np.maximum(np.where(amax > 0, np.frexp(amax)[1] - 1 + 127, 0) - down, 1)
    scale = np.exp2(byte - 127.0)
    codes = (blocks / scale).astype(np.float32).astype(dtype).astype(np.float64)
    return np.moveaxis((codes * scale).reshape(v.shape), -1, axis)


WIDE = False


def mx_kscale(k, group=512):
    if not WIDE:
        return np.ones(k)
    levels = np.array([10, -10, 5, -5, 0])
    if group != 512:
        return np.exp2(np.random.permutation(np.resize(levels, k // group))).repeat(group)
    if k % 512:
        return np.exp2(np.random.permutation(np.resize(levels, k // 32))).repeat(32)
    a = np.empty((k // 512, 16))
    for p in range(k // 512):
        a[p, :8] = np.random.permutation(np.resize(levels, 8))
        for g in range(8):
            far = levels[np.abs(levels - a[p, g]) >= 10]
            a[p, g + 8] = far[np.random.randint(len(far))]
    return np.exp2(a.ravel()).repeat(32)


def f64(x):
    return np.asarray(x).astype(np.float64)


G, D, K, M, N = 2, 256, 1024, 256, 512


def setup_inputs():
    n = np.random.standard_normal
    s = mx_kscale(D, 0)[:, None]
    u = mx_kscale(K)[:, None]
    return {
        "x": (n((G, D, N)) * s).astype(np.float32),
        "w1": (n((G, D, K)) / np.sqrt(D) / s).astype(np.float32),
        "hs": (np.random.uniform(0.5, 2.0, (G, K, 1)) * u).astype(np.float32),
        "w2": (n((G, K, M)) / np.sqrt(K) / u).astype(np.float32),
        "b": (0.5 * n((G, K, 1))).astype(np.float32),
        "r": n((G, M, N)).astype(np.float32),
    }


def reference(x, w1, hs, w2, b, r):
    xq = mxq(f64(x), 1, "e4m3")
    h = mxq(f64(w1), 1, "e4m3").transpose(0, 2, 1) @ xq
    h = h + f64(b)
    h = (np.maximum(h, 0.0)) * f64(hs)
    y = mxq(f64(w2), 1, "e4m3").transpose(0, 2, 1) @ mxq(h, 1, "e4m3")
    y = y + f64(r)
    return y

@@ -1,0 +1,259 @@
+from contextlib import ExitStack
+
+import concourse.mybir as mybir
+
+G, D, K, M, N = 2, 256, 1024, 256, 512
+FLOPS = 2 * G * D * K * N + 2 * G * K * M * N
+
+F32 = mybir.dt.float32
+BF16 = mybir.dt.bfloat16
+U32 = mybir.dt.uint32
+U8 = mybir.dt.uint8
+FP8X4 = mybir.dt.float8_e4m3fn_x4
+ACT = mybir.ActivationFunctionType
+ALU = mybir.AluOpType
+
+P = 128
+PACK = 4
+ROWS = D // PACK
+K_PASS = P * PACK
+PASSES = K // K_PASS
+HALF = K_PASS // 2
+M_TILES = M // P
+Z_BANKS = 2
+
+PAIRED = (False, True, True, True)
+X_VECTOR = 352
+W_FIRST_VECTOR = 32
+W_SECOND_VECTOR = 44
+
+
+def tile_rows_gmlp_relu_bias_res_kernel(tc, x, w1, hs, w2, b, r, out):
+    nc = tc.nc
+    with ExitStack() as ctx:
+        sb = ctx.enter_context(tc.tile_pool(name="sb", bufs=1))
+        ps = ctx.enter_context(tc.psum_pool(name="ps", bufs=1))
+        ctx.enter_context(tc.manual_schedule())
+
+        def tile(name, shape, dtype):
+            return sb.tile(shape, dtype, name=name, align_bytes=64)
+
+        units = [(g, c) for c in range(PASSES) for g in range(G)]
+
+        hs_sb = tile("hs_sb", [P, G * PASSES, PACK], F32)
+        b_sb = tile("b_sb", [P, G * PASSES, PACK], F32)
+        hs_abs = tile("hs_abs", [P, G * PASSES, PACK], F32)
+        hs_sign = tile("hs_sign", [P, G * PASSES, PACK], F32)
+        bias = tile("bias", [P, G * PASSES, PACK], F32)
+
+        x_raw = tile("x_raw", [P, PACK, N], F32)
+        x_bf = tile("x_bf", [P, N, PACK], BF16)
+        x_codes = tile("x_codes", [P, N], U32)
+        x_scales = tile("x_scales", [P, N], U8)
+        w1_raw = [[tile("w1_raw%d%d" % (c, h), [P, PACK, HALF], F32) for h in range(2)] for c in range(PASSES)]
+        w1_bf = [tile("w1_bf%d" % c, [P, PACK, P, PACK], BF16) for c in range(PASSES)]
+        w1_codes = [tile("w1_codes%d" % c, [P, K_PASS], U32) for c in range(PASSES)]
+        w1_scales = [tile("w1_scales%d" % c, [P, K_PASS], U8) for c in range(PASSES)]
+        w2_raw = [tile("w2_raw%d" % u, [P, PACK, M], F32) for u in range(4)]
+        w2_bf = [tile("w2_bf%d" % u, [P, M, PACK], BF16) for u in range(4)]
+        w2_codes = [tile("w2_codes%d" % u, [P, M], U32) for u in range(4)]
+        w2_scales = [tile("w2_scales%d" % u, [P, M], U8) for u in range(4)]
+        h_out = [tile("h_out%d" % u, [P, PACK * N], BF16) for u in range(4)]
+        h_bf = [tile("h_bf%d" % u, [P, N, PACK], BF16) for u in range(4)]
+        h_codes = [tile("h_codes%d" % u, [P, N], U32) for u in range(4)]
+        h_scales = [tile("h_scales%d" % u, [P, N], U8) for u in range(4)]
+        r_sb = [tile("r_sb%d" % g, [P, M_TILES, N], F32) for g in range(G)]
+        res = [[tile("res%d%d" % (g, t), [P, N], F32) for t in range(M_TILES)] for g in range(G)]
+        z_ps = [[ps.tile([P, N], F32, name="z%d%d" % (g, i)) for i in range(Z_BANKS)] for g in range(G)]
+        y_ps = [[ps.tile([P, N], F32, name="y%d%d" % (g, t)) for t in range(M_TILES)] for g in range(G)]
+
+        nc.sync.dma_start(out=hs_sb[:], in_=hs.rearrange("g (c p t) o -> p (g c) (t o)", p=P, t=PACK))
+        nc.sync.dma_start(out=b_sb[:], in_=b.rearrange("g (c p t) o -> p (g c) (t o)", p=P, t=PACK))
+        nc.sync.dma_start(out=x_raw[:], in_=x.rearrange("g (q j) n -> (g q) j n", j=PACK))
+        w1_rows = w1.rearrange("g (q j) k -> (g q) j k", j=PACK)
+
+        def load_w1(c, h):
+            k0 = c * K_PASS + h * HALF
+            nc.sync.dma_start(out=w1_raw[c][h][:], in_=w1_rows[:, :, k0 : k0 + HALF])
+
+        def load_w2(u):
+            g, c = units[u]
+            nc.sync.dma_start(
+                out=w2_raw[u][:],
+                in_=w2[g, c * K_PASS : (c + 1) * K_PASS, :].rearrange("(p j) m -> p j m", j=PACK),
+            )
+
+        def load_r(g):
+            nc.sync.dma_start(out=r_sb[g][:], in_=r[g].rearrange("(t p) n -> p t n", p=P))
+
+        load_w1(0, 0)
+        load_w1(0, 1)
+        load_w2(0)
+        load_w1(1, 0)
+        load_w1(1, 1)
+        load_w2(1)
+        load_w2(2)
+        load_w2(3)
+        load_r(0)
+        load_r(1)
+
+        def entry(u):
+            g, c = units[u]
+            return g * PASSES + c
+
+        def quantize(codes, scales, values):
+            nc.vector.quantize_mx(out=codes.bitcast(FP8X4), scales=scales, in_=values)
+
+        def cast_x(copy, n0, n1):
+            copy(
+                out=x_bf[:, n0:n1, :].rearrange("p (c i) j -> p c j i", i=2),
+                in_=x_raw[:, :, n0:n1].rearrange("p j (c i) -> p c j i", i=2),
+            )
+
+        def cast_w1(copy, c, h, m0, m1):
+            base = h * (P // 2)
+            copy(
+                out=w1_bf[c][:, :, base + m0 : base + m1, :].rearrange("p t m j -> p m j t"),
+                in_=w1_raw[c][h][:, :, PACK * m0 : PACK * m1].rearrange("p j (m t) -> p m j t", t=PACK),
+            )
+
+        def quantize_w1(c, t0, t1):
+            cols = slice(t0 * P, t1 * P)
+            quantize(w1_codes[c][:, cols], w1_scales[c][:, cols], w1_bf[c][:, t0:t1, :, :].rearrange("p t m j -> p (t m j)"))
+
+        def cast_w2(u):
+            nc.vector.tensor_tensor(
+                out=w2_bf[u][:].rearrange("p (c i) j -> p c j i", i=2),
+                in0=w2_raw[u][:].rearrange("p j (c i) -> p c j i", i=2),
+                in1=hs_sign[:, entry(u), :].unsqueeze(1).unsqueeze(3).to_broadcast([P, M // 2, PACK, 2]),
+                op=ALU.mult,
+            )
+
+        def quantize_w2(u):
+            quantize(w2_codes[u][:], w2_scales[u][:], w2_bf[u][:].rearrange("p m j -> p (m j)"))
+
+        def z_bank(u, t):
+            g, c = units[u]
+            return z_ps[g][(c * PACK + t) % Z_BANKS]
+
+        def first_product(u, t):
+            g, c = units[u]
+            rows = slice(g * ROWS, (g + 1) * ROWS)
+            cols = slice(t * P, (t + 1) * P)
+            nc.tensor.matmul_mx(
+                out=z_bank(u, t)[:],
+                lhsT=w1_codes[c][rows, cols].bitcast(FP8X4),
+                lhsT_scale=w1_scales[c][rows, cols],
+                rhs=x_codes[rows, :].bitcast(FP8X4),
+                rhs_scale=x_scales[rows, :],
+                start=True,
+                stop=True,
+            )
+
+        def activate(u, t):
+            if PAIRED[u]:
+                dst = h_out[u][:].rearrange("p (v n e) -> p v n e", v=2, e=2)[:, t // 2, :, t % 2]
+            else:
+                dst = h_out[u][:, t * N : (t + 1) * N]
+            nc.scalar.activation(
+                out=dst,
+                in_=z_bank(u, t)[:],
+                func=ACT.Relu,
+                scale=hs_abs[:, entry(u), t : t + 1],
+                bias=bias[:, entry(u), t : t + 1],
+            )
+
+        def interleave_h(u):
+            if PAIRED[u]:
+                nc.vector.tensor_copy(
+                    out=h_bf[u][:].rearrange("p n (v e) -> p n v e", e=2),
+                    in_=h_out[u][:].rearrange("p (v n e) -> p n v e", v=2, e=2),
+                )
+            else:
+                nc.vector.tensor_copy(
+                    out=h_bf[u][:].rearrange("p (c i) t -> p c t i", i=4),
+                    in_=h_out[u][:].rearrange("p (t c i) -> p c t i", t=PACK, i=4),
+                )
+
+        def quantize_h(u):
+            quantize(h_codes[u][:], h_scales[u][:], h_bf[u][:].rearrange("p n t -> p (n t)"))
+
+        def second_product(u):
+            g, c = units[u]
+            for t in range(M_TILES):
+                cols = slice(t * P, (t + 1) * P)
+                nc.tensor.matmul_mx(
+                    out=y_ps[g][t][:],
+                    lhsT=w2_codes[u][:, cols].bitcast(FP8X4),
+                    lhsT_scale=w2_scales[u][:, cols],
+                    rhs=h_codes[u][:].bitcast(FP8X4),
+                    rhs_scale=h_scales[u][:],
+                    start=(c == 0),
+                    stop=(c == PASSES - 1),
+                )
+
+        def finish(g, t):
+            nc.vector.tensor_tensor(out=res[g][t][:], in0=y_ps[g][t][:], in1=r_sb[g][:, t, :], op=ALU.add)
+            nc.sync.dma_start(out=out[g, t * P : (t + 1) * P, :], in_=res[g][t][:])
+
+        vcopy = nc.vector.tensor_copy
+        scopy = nc.scalar.copy
+
+        def first_layer(u):
+            for t in range(PACK):
+                if t >= Z_BANKS:
+                    first_product(u, t)
+                activate(u, t)
+
+        def prefetch(u):
+            for t in range(Z_BANKS):
+                first_product(u, t)
+
+        nc.scalar.activation(out=hs_abs[:], in_=hs_sb[:], func=ACT.Abs)
+        nc.scalar.activation(out=hs_sign[:], in_=hs_sb[:], func=ACT.Sign)
+        nc.gpsimd.tensor_tensor(out=bias[:], in0=hs_abs[:], in1=b_sb[:], op=ALU.mult)
+        cast_x(vcopy, 0, X_VECTOR)
+        cast_x(scopy, X_VECTOR, N)
+        quantize(x_codes[:], x_scales[:], x_bf[:].rearrange("p n j -> p (n j)"))
+        cast_w1(scopy, 0, 0, W_FIRST_VECTOR, P // 2)
+        cast_w1(vcopy, 0, 0, 0, W_FIRST_VECTOR)
+        cast_w1(vcopy, 0, 1, 0, W_SECOND_VECTOR)
+        cast_w1(scopy, 0, 1, W_SECOND_VECTOR, P // 2)
+        quantize_w1(0, 0, 1)
+        quantize_w1(0, 1, 2)
+        quantize_w1(0, 2, 4)
+        prefetch(0)
+        prefetch(1)
+        first_layer(0)
+        first_layer(1)
+        cast_w2(0)
+        cast_w1(vcopy, 1, 0, 0, P // 2)
+        quantize_w2(0)
+        cast_w1(vcopy, 1, 1, 0, P // 2)
+        interleave_h(0)
+        quantize_w1(1, 0, 4)
+        prefetch(2)
+        quantize_h(0)
+        second_product(0)
+        prefetch(3)
+        first_layer(2)
+        cast_w2(1)
+        interleave_h(1)
+        quantize_w2(1)
+        quantize_h(1)
+        second_product(1)
+        first_layer(3)
+        cast_w2(2)
+        quantize_w2(2)
+        interleave_h(2)
+        cast_w2(3)
+        quantize_h(2)
+        second_product(2)
+        quantize_w2(3)
+        finish(0, 0)
+        interleave_h(3)
+        quantize_h(3)
+        second_product(3)
+        finish(0, 1)
+        finish(1, 0)
+        finish(1, 1)

@@ -22,7 +22,8 @@ HALF = K_PASS // 2
 M_TILES = M // P
 Z_BANKS = 2
 
-PAIRED = (False, True, True, True)
+PAIRED = (True, True, False, True)
+H_LAST_VECTOR = 320
 X_VECTOR = 352
 W_FIRST_VECTOR = 32
 W_SECOND_VECTOR = 44
@@ -38,7 +39,7 @@ def tile_rows_gmlp_relu_bias_res_kernel(tc, x, w1, hs, w2, b, r, out):
         def tile(name, shape, dtype):
             return sb.tile(shape, dtype, name=name, align_bytes=64)
 
-        units = [(g, c) for c in range(PASSES) for g in range(G)]
+        units = [(g, c) for g in range(G) for c in range(PASSES)]
 
         hs_sb = tile("hs_sb", [P, G * PASSES, PACK], F32)
         b_sb = tile("b_sb", [P, G * PASSES, PACK], F32)
@@ -67,8 +68,6 @@ def tile_rows_gmlp_relu_bias_res_kernel(tc, x, w1, hs, w2, b, r, out):
         z_ps = [[ps.tile([P, N], F32, name="z%d%d" % (g, i)) for i in range(Z_BANKS)] for g in range(G)]
         y_ps = [[ps.tile([P, N], F32, name="y%d%d" % (g, t)) for t in range(M_TILES)] for g in range(G)]
 
-        nc.sync.dma_start(out=hs_sb[:], in_=hs.rearrange("g (c p t) o -> p (g c) (t o)", p=P, t=PACK))
-        nc.sync.dma_start(out=b_sb[:], in_=b.rearrange("g (c p t) o -> p (g c) (t o)", p=P, t=PACK))
         nc.sync.dma_start(out=x_raw[:], in_=x.rearrange("g (q j) n -> (g q) j n", j=PACK))
         w1_rows = w1.rearrange("g (q j) k -> (g q) j k", j=PACK)
 
@@ -88,6 +87,8 @@ def tile_rows_gmlp_relu_bias_res_kernel(tc, x, w1, hs, w2, b, r, out):
 
         load_w1(0, 0)
         load_w1(0, 1)
+        nc.sync.dma_start(out=hs_sb[:], in_=hs.rearrange("g (c p t) o -> p (g c) (t o)", p=P, t=PACK))
+        nc.sync.dma_start(out=b_sb[:], in_=b.rearrange("g (c p t) o -> p (g c) (t o)", p=P, t=PACK))
         load_w2(0)
         load_w1(1, 0)
         load_w1(1, 1)
@@ -163,16 +164,16 @@ def tile_rows_gmlp_relu_bias_res_kernel(tc, x, w1, hs, w2, b, r, out):
                 bias=bias[:, entry(u), t : t + 1],
             )
 
-        def interleave_h(u):
+        def interleave_h(copy, u, n0, n1):
             if PAIRED[u]:
-                nc.vector.tensor_copy(
-                    out=h_bf[u][:].rearrange("p n (v e) -> p n v e", e=2),
-                    in_=h_out[u][:].rearrange("p (v n e) -> p n v e", v=2, e=2),
+                copy(
+                    out=h_bf[u][:, n0:n1, :].rearrange("p n (v e) -> p n v e", e=2),
+                    in_=h_out[u][:].rearrange("p (v n e) -> p n v e", v=2, e=2)[:, n0:n1, :, :],
                 )
             else:
-                nc.vector.tensor_copy(
-                    out=h_bf[u][:].rearrange("p (c i) t -> p c t i", i=4),
-                    in_=h_out[u][:].rearrange("p (t c i) -> p c t i", t=PACK, i=4),
+                copy(
+                    out=h_bf[u][:, n0:n1, :].rearrange("p (c i) t -> p c t i", i=4),
+                    in_=h_out[u][:].rearrange("p (t n) -> p t n", t=PACK)[:, :, n0:n1].rearrange("p t (c i) -> p c t i", i=4),
                 )
 
         def quantize_h(u):
@@ -199,59 +200,74 @@ def tile_rows_gmlp_relu_bias_res_kernel(tc, x, w1, hs, w2, b, r, out):
         vcopy = nc.vector.tensor_copy
         scopy = nc.scalar.copy
 
-        def first_layer(u):
-            for t in range(PACK):
-                if t >= Z_BANKS:
-                    first_product(u, t)
-                activate(u, t)
-
-        def prefetch(u):
-            for t in range(Z_BANKS):
-                first_product(u, t)
-
-        nc.scalar.activation(out=hs_abs[:], in_=hs_sb[:], func=ACT.Abs)
-        nc.scalar.activation(out=hs_sign[:], in_=hs_sb[:], func=ACT.Sign)
-        nc.gpsimd.tensor_tensor(out=bias[:], in0=hs_abs[:], in1=b_sb[:], op=ALU.mult)
         cast_x(vcopy, 0, X_VECTOR)
         cast_x(scopy, X_VECTOR, N)
-        quantize(x_codes[:], x_scales[:], x_bf[:].rearrange("p n j -> p (n j)"))
-        cast_w1(scopy, 0, 0, W_FIRST_VECTOR, P // 2)
         cast_w1(vcopy, 0, 0, 0, W_FIRST_VECTOR)
+        cast_w1(scopy, 0, 0, W_FIRST_VECTOR, P // 2)
+        quantize(x_codes[:], x_scales[:], x_bf[:].rearrange("p n j -> p (n j)"))
         cast_w1(vcopy, 0, 1, 0, W_SECOND_VECTOR)
         cast_w1(scopy, 0, 1, W_SECOND_VECTOR, P // 2)
+        nc.scalar.activation(out=hs_abs[:], in_=hs_sb[:], func=ACT.Abs)
+        nc.scalar.activation(out=hs_sign[:], in_=hs_sb[:], func=ACT.Sign)
         quantize_w1(0, 0, 1)
         quantize_w1(0, 1, 2)
+        nc.vector.tensor_tensor(out=bias[:], in0=hs_abs[:], in1=b_sb[:], op=ALU.mult)
         quantize_w1(0, 2, 4)
-        prefetch(0)
-        prefetch(1)
-        first_layer(0)
-        first_layer(1)
+        first_product(0, 0)
+        first_product(0, 1)
+        first_product(2, 0)
+        activate(0, 0)
+        first_product(0, 2)
+        activate(0, 1)
+        first_product(0, 3)
+        first_product(2, 1)
+        activate(2, 0)
         cast_w2(0)
         cast_w1(vcopy, 1, 0, 0, P // 2)
         quantize_w2(0)
         cast_w1(vcopy, 1, 1, 0, P // 2)
-        interleave_h(0)
         quantize_w1(1, 0, 4)
-        prefetch(2)
+        activate(0, 2)
+        first_product(1, 0)
+        activate(0, 3)
+        first_product(1, 1)
+        first_product(2, 2)
+        activate(2, 1)
+        activate(1, 0)
+        first_product(1, 2)
+        first_product(2, 3)
+        activate(1, 1)
+        first_product(1, 3)
+        activate(2, 2)
+        first_product(3, 0)
+        cast_w2(1)
+        interleave_h(vcopy, 0, 0, N)
+        cast_w2(2)
         quantize_h(0)
         second_product(0)
-        prefetch(3)
-        first_layer(2)
-        cast_w2(1)
-        interleave_h(1)
+        activate(1, 2)
+        activate(1, 3)
+        activate(2, 3)
+        first_product(3, 1)
+        activate(3, 0)
+        first_product(3, 2)
+        activate(3, 1)
+        first_product(3, 3)
+        activate(3, 2)
+        activate(3, 3)
         quantize_w2(1)
+        cast_w2(3)
+        quantize_w2(2)
+        interleave_h(vcopy, 1, 0, N)
+        interleave_h(vcopy, 2, 0, N)
         quantize_h(1)
         second_product(1)
-        first_layer(3)
-        cast_w2(2)
-        quantize_w2(2)
-        interleave_h(2)
-        cast_w2(3)
         quantize_h(2)
         second_product(2)
         quantize_w2(3)
+        interleave_h(vcopy, 3, 0, H_LAST_VECTOR)
+        interleave_h(scopy, 3, H_LAST_VECTOR, N)
         finish(0, 0)
-        interleave_h(3)
         quantize_h(3)
         second_product(3)
         finish(0, 1)

@@ -21,12 +21,13 @@ PASSES = K // K_PASS
 HALF = K_PASS // 2
 M_TILES = M // P
 Z_BANKS = 2
+QUAD = 32
 
 PAIRED = (True, True, False, True)
-H_LAST_VECTOR = 320
+H_LAST_VECTOR = 288
 X_VECTOR = 352
 W_FIRST_VECTOR = 32
-W_SECOND_VECTOR = 44
+W_SECOND_VECTOR = 40
 
 
 def tile_rows_gmlp_relu_bias_res_kernel(tc, x, w1, hs, w2, b, r, out):
@@ -41,8 +42,9 @@ def tile_rows_gmlp_relu_bias_res_kernel(tc, x, w1, hs, w2, b, r, out):
 
         units = [(g, c) for g in range(G) for c in range(PASSES)]
 
-        hs_sb = tile("hs_sb", [P, G * PASSES, PACK], F32)
-        b_sb = tile("b_sb", [P, G * PASSES, PACK], F32)
+        rows_in = tile("rows_in", [P, G * PASSES, QUAD, PACK], F32)
+        rows_dealt = tile("rows_dealt", [P, G * PASSES, PACK, QUAD], F32)
+        rows_turned = tile("rows_turned", [P, G * PASSES * PACK, QUAD], F32)
         hs_abs = tile("hs_abs", [P, G * PASSES, PACK], F32)
         hs_sign = tile("hs_sign", [P, G * PASSES, PACK], F32)
         bias = tile("bias", [P, G * PASSES, PACK], F32)
@@ -68,6 +70,12 @@ def tile_rows_gmlp_relu_bias_res_kernel(tc, x, w1, hs, w2, b, r, out):
         z_ps = [[ps.tile([P, N], F32, name="z%d%d" % (g, i)) for i in range(Z_BANKS)] for g in range(G)]
         y_ps = [[ps.tile([P, N], F32, name="y%d%d" % (g, t)) for t in range(M_TILES)] for g in range(G)]
 
+        nc.vector.memset(rows_in[:], 0.0)
+        for row, vec in enumerate((hs, b)):
+            nc.scalar.dma_start(
+                out=rows_in[row:P:QUAD, :, :, :].rearrange("q e i t -> q e (i t)"),
+                in_=vec.rearrange("g (c q f) o -> q (g c) (f o)", c=PASSES, q=P // QUAD),
+            )
         nc.sync.dma_start(out=x_raw[:], in_=x.rearrange("g (q j) n -> (g q) j n", j=PACK))
         w1_rows = w1.rearrange("g (q j) k -> (g q) j k", j=PACK)
 
@@ -87,8 +95,6 @@ def tile_rows_gmlp_relu_bias_res_kernel(tc, x, w1, hs, w2, b, r, out):
 
         load_w1(0, 0)
         load_w1(0, 1)
-        nc.sync.dma_start(out=hs_sb[:], in_=hs.rearrange("g (c p t) o -> p (g c) (t o)", p=P, t=PACK))
-        nc.sync.dma_start(out=b_sb[:], in_=b.rearrange("g (c p t) o -> p (g c) (t o)", p=P, t=PACK))
         load_w2(0)
         load_w1(1, 0)
         load_w1(1, 1)
@@ -200,18 +206,27 @@ def tile_rows_gmlp_relu_bias_res_kernel(tc, x, w1, hs, w2, b, r, out):
         vcopy = nc.vector.tensor_copy
         scopy = nc.scalar.copy
 
+        nc.vector.tensor_copy(out=rows_dealt[:], in_=rows_in[:].rearrange("p e i t -> p e t i"))
+        nc.vector.transpose(
+            out=rows_turned[:].rearrange("p e r -> p (e r)"), in_=rows_dealt[:].rearrange("p e t i -> p (e t i)")
+        )
         cast_x(vcopy, 0, X_VECTOR)
         cast_x(scopy, X_VECTOR, N)
+        nc.scalar.activation(out=hs_abs[:].rearrange("p e t -> p (e t)"), in_=rows_turned[:, :, 0], func=ACT.Abs)
+        nc.scalar.activation(out=hs_sign[:].rearrange("p e t -> p (e t)"), in_=rows_turned[:, :, 0], func=ACT.Sign)
         cast_w1(vcopy, 0, 0, 0, W_FIRST_VECTOR)
         cast_w1(scopy, 0, 0, W_FIRST_VECTOR, P // 2)
+        nc.vector.tensor_tensor(
+            out=bias[:].rearrange("p e t -> p (e t)"),
+            in0=hs_abs[:].rearrange("p e t -> p (e t)"),
+            in1=rows_turned[:, :, 1],
+            op=ALU.mult,
+        )
         quantize(x_codes[:], x_scales[:], x_bf[:].rearrange("p n j -> p (n j)"))
         cast_w1(vcopy, 0, 1, 0, W_SECOND_VECTOR)
         cast_w1(scopy, 0, 1, W_SECOND_VECTOR, P // 2)
-        nc.scalar.activation(out=hs_abs[:], in_=hs_sb[:], func=ACT.Abs)
-        nc.scalar.activation(out=hs_sign[:], in_=hs_sb[:], func=ACT.Sign)
         quantize_w1(0, 0, 1)
         quantize_w1(0, 1, 2)
-        nc.vector.tensor_tensor(out=bias[:], in0=hs_abs[:], in1=b_sb[:], op=ALU.mult)
         quantize_w1(0, 2, 4)
         first_product(0, 0)
         first_product(0, 1)

@@ -24,10 +24,10 @@ Z_BANKS = 2
 QUAD = 32
 
 PAIRED = (True, True, False, True)
-H_LAST_VECTOR = 288
-X_VECTOR = 352
-W_FIRST_VECTOR = 32
-W_SECOND_VECTOR = 40
+H_LAST_VECTOR = 320
+X_VECTOR = 288
+W_FIRST_VECTOR = 24
+W_SECOND_VECTOR = 44
 
 
 def tile_rows_gmlp_relu_bias_res_kernel(tc, x, w1, hs, w2, b, r, out):
@@ -42,7 +42,7 @@ def tile_rows_gmlp_relu_bias_res_kernel(tc, x, w1, hs, w2, b, r, out):
 
         units = [(g, c) for g in range(G) for c in range(PASSES)]
 
-        rows_in = tile("rows_in", [P, G * PASSES, QUAD, PACK], F32)
+        rows_in = tile("rows_in", [P, 2, G * PASSES, QUAD, PACK], F32)
         rows_dealt = tile("rows_dealt", [P, G * PASSES, PACK, QUAD], F32)
         rows_turned = tile("rows_turned", [P, G * PASSES * PACK, QUAD], F32)
         hs_abs = tile("hs_abs", [P, G * PASSES, PACK], F32)
@@ -71,12 +71,12 @@ def tile_rows_gmlp_relu_bias_res_kernel(tc, x, w1, hs, w2, b, r, out):
         y_ps = [[ps.tile([P, N], F32, name="y%d%d" % (g, t)) for t in range(M_TILES)] for g in range(G)]
 
         nc.vector.memset(rows_in[:], 0.0)
+        nc.sync.dma_start(out=x_raw[:], in_=x.rearrange("g (q j) n -> (g q) j n", j=PACK))
         for row, vec in enumerate((hs, b)):
-            nc.scalar.dma_start(
-                out=rows_in[row:P:QUAD, :, :, :].rearrange("q e i t -> q e (i t)"),
+            nc.sync.dma_start(
+                out=rows_in[row:P:QUAD, row, :, :, :].rearrange("q e i t -> q e (i t)"),
                 in_=vec.rearrange("g (c q f) o -> q (g c) (f o)", c=PASSES, q=P // QUAD),
             )
-        nc.sync.dma_start(out=x_raw[:], in_=x.rearrange("g (q j) n -> (g q) j n", j=PACK))
         w1_rows = w1.rearrange("g (q j) k -> (g q) j k", j=PACK)
 
         def load_w1(c, h):
@@ -206,27 +206,32 @@ def tile_rows_gmlp_relu_bias_res_kernel(tc, x, w1, hs, w2, b, r, out):
         vcopy = nc.vector.tensor_copy
         scopy = nc.scalar.copy
 
-        nc.vector.tensor_copy(out=rows_dealt[:], in_=rows_in[:].rearrange("p e i t -> p e t i"))
+        cast_x(vcopy, 0, X_VECTOR)
+        cast_x(scopy, X_VECTOR, N)
+        nc.vector.tensor_tensor(
+            out=rows_dealt[:].rearrange("p e t i -> p e i t"),
+            in0=rows_in[:, 0, :, :, :],
+            in1=rows_in[:, 1, :, :, :],
+            op=ALU.add,
+        )
+        quantize(x_codes[:], x_scales[:], x_bf[:].rearrange("p n j -> p (n j)"))
         nc.vector.transpose(
             out=rows_turned[:].rearrange("p e r -> p (e r)"), in_=rows_dealt[:].rearrange("p e t i -> p (e t i)")
         )
-        cast_x(vcopy, 0, X_VECTOR)
-        cast_x(scopy, X_VECTOR, N)
+        cast_w1(scopy, 0, 0, W_FIRST_VECTOR, P // 2)
+        cast_w1(vcopy, 0, 0, 0, W_FIRST_VECTOR)
+        cast_w1(vcopy, 0, 1, 0, W_SECOND_VECTOR)
+        cast_w1(scopy, 0, 1, W_SECOND_VECTOR, P // 2)
         nc.scalar.activation(out=hs_abs[:].rearrange("p e t -> p (e t)"), in_=rows_turned[:, :, 0], func=ACT.Abs)
         nc.scalar.activation(out=hs_sign[:].rearrange("p e t -> p (e t)"), in_=rows_turned[:, :, 0], func=ACT.Sign)
-        cast_w1(vcopy, 0, 0, 0, W_FIRST_VECTOR)
-        cast_w1(scopy, 0, 0, W_FIRST_VECTOR, P // 2)
+        quantize_w1(0, 0, 1)
+        quantize_w1(0, 1, 2)
         nc.vector.tensor_tensor(
             out=bias[:].rearrange("p e t -> p (e t)"),
             in0=hs_abs[:].rearrange("p e t -> p (e t)"),
             in1=rows_turned[:, :, 1],
             op=ALU.mult,
         )
-        quantize(x_codes[:], x_scales[:], x_bf[:].rearrange("p n j -> p (n j)"))
-        cast_w1(vcopy, 0, 1, 0, W_SECOND_VECTOR)
-        cast_w1(scopy, 0, 1, W_SECOND_VECTOR, P // 2)
-        quantize_w1(0, 0, 1)
-        quantize_w1(0, 1, 2)
         quantize_w1(0, 2, 4)
         first_product(0, 0)
         first_product(0, 1)

from contextlib import ExitStack

import concourse.mybir as mybir

G, D, K, M, N = 2, 256, 1024, 256, 512
FLOPS = 2 * G * D * K * N + 2 * G * K * M * N

F32 = mybir.dt.float32
BF16 = mybir.dt.bfloat16
U32 = mybir.dt.uint32
U8 = mybir.dt.uint8
FP8X4 = mybir.dt.float8_e4m3fn_x4
ACT = mybir.ActivationFunctionType
ALU = mybir.AluOpType

P = 128
PACK = 4
ROWS = D // PACK
K_PASS = P * PACK
PASSES = K // K_PASS
HALF = K_PASS // 2
M_TILES = M // P
Z_BANKS = 2
QUAD = 32

PAIRED = (True, True, False, True)
H_LAST_VECTOR = 320
X_VECTOR = 288
W_FIRST_VECTOR = 24
W_SECOND_VECTOR = 44


def tile_rows_gmlp_relu_bias_res_kernel(tc, x, w1, hs, w2, b, r, out):
    nc = tc.nc
    with ExitStack() as ctx:
        sb = ctx.enter_context(tc.tile_pool(name="sb", bufs=1))
        ps = ctx.enter_context(tc.psum_pool(name="ps", bufs=1))
        ctx.enter_context(tc.manual_schedule())

        def tile(name, shape, dtype):
            return sb.tile(shape, dtype, name=name, align_bytes=64)

        units = [(g, c) for g in range(G) for c in range(PASSES)]

        rows_in = tile("rows_in", [P, 2, G * PASSES, QUAD, PACK], F32)
        rows_dealt = tile("rows_dealt", [P, G * PASSES, PACK, QUAD], F32)
        rows_turned = tile("rows_turned", [P, G * PASSES * PACK, QUAD], F32)
        hs_abs = tile("hs_abs", [P, G * PASSES, PACK], F32)
        hs_sign = tile("hs_sign", [P, G * PASSES, PACK], F32)
        bias = tile("bias", [P, G * PASSES, PACK], F32)

        x_raw = tile("x_raw", [P, PACK, N], F32)
        x_bf = tile("x_bf", [P, N, PACK], BF16)
        x_codes = tile("x_codes", [P, N], U32)
        x_scales = tile("x_scales", [P, N], U8)
        w1_raw = [[tile("w1_raw%d%d" % (c, h), [P, PACK, HALF], F32) for h in range(2)] for c in range(PASSES)]
        w1_bf = [tile("w1_bf%d" % c, [P, PACK, P, PACK], BF16) for c in range(PASSES)]
        w1_codes = [tile("w1_codes%d" % c, [P, K_PASS], U32) for c in range(PASSES)]
        w1_scales = [tile("w1_scales%d" % c, [P, K_PASS], U8) for c in range(PASSES)]
        w2_raw = [tile("w2_raw%d" % u, [P, PACK, M], F32) for u in range(4)]
        w2_bf = [tile("w2_bf%d" % u, [P, M, PACK], BF16) for u in range(4)]
        w2_codes = [tile("w2_codes%d" % u, [P, M], U32) for u in range(4)]
        w2_scales = [tile("w2_scales%d" % u, [P, M], U8) for u in range(4)]
        h_out = [tile("h_out%d" % u, [P, PACK * N], BF16) for u in range(4)]
        h_bf = [tile("h_bf%d" % u, [P, N, PACK], BF16) for u in range(4)]
        h_codes = [tile("h_codes%d" % u, [P, N], U32) for u in range(4)]
        h_scales = [tile("h_scales%d" % u, [P, N], U8) for u in range(4)]
        r_sb = [tile("r_sb%d" % g, [P, M_TILES, N], F32) for g in range(G)]
        res = [[tile("res%d%d" % (g, t), [P, N], F32) for t in range(M_TILES)] for g in range(G)]
        z_ps = [[ps.tile([P, N], F32, name="z%d%d" % (g, i)) for i in range(Z_BANKS)] for g in range(G)]
        y_ps = [[ps.tile([P, N], F32, name="y%d%d" % (g, t)) for t in range(M_TILES)] for g in range(G)]

        nc.vector.memset(rows_in[:], 0.0)
        nc.sync.dma_start(out=x_raw[:], in_=x.rearrange("g (q j) n -> (g q) j n", j=PACK))
        for row, vec in enumerate((hs, b)):
            nc.sync.dma_start(
                out=rows_in[row:P:QUAD, row, :, :, :].rearrange("q e i t -> q e (i t)"),
                in_=vec.rearrange("g (c q f) o -> q (g c) (f o)", c=PASSES, q=P // QUAD),
            )
        w1_rows = w1.rearrange("g (q j) k -> (g q) j k", j=PACK)

        def load_w1(c, h):
            k0 = c * K_PASS + h * HALF
            nc.sync.dma_start(out=w1_raw[c][h][:], in_=w1_rows[:, :, k0 : k0 + HALF])

        def load_w2(u):
            g, c = units[u]
            nc.sync.dma_start(
                out=w2_raw[u][:],
                in_=w2[g, c * K_PASS : (c + 1) * K_PASS, :].rearrange("(p j) m -> p j m", j=PACK),
            )

        def load_r(g):
            nc.sync.dma_start(out=r_sb[g][:], in_=r[g].rearrange("(t p) n -> p t n", p=P))

        load_w1(0, 0)
        load_w1(0, 1)
        load_w2(0)
        load_w1(1, 0)
        load_w1(1, 1)
        load_w2(1)
        load_w2(2)
        load_w2(3)
        load_r(0)
        load_r(1)

        def entry(u):
            g, c = units[u]
            return g * PASSES + c

        def quantize(codes, scales, values):
            nc.vector.quantize_mx(out=codes.bitcast(FP8X4), scales=scales, in_=values)

        def cast_x(copy, n0, n1):
            copy(
                out=x_bf[:, n0:n1, :].rearrange("p (c i) j -> p c j i", i=2),
                in_=x_raw[:, :, n0:n1].rearrange("p j (c i) -> p c j i", i=2),
            )

        def cast_w1(copy, c, h, m0, m1):
            base = h * (P // 2)
            copy(
                out=w1_bf[c][:, :, base + m0 : base + m1, :].rearrange("p t m j -> p m j t"),
                in_=w1_raw[c][h][:, :, PACK * m0 : PACK * m1].rearrange("p j (m t) -> p m j t", t=PACK),
            )

        def quantize_w1(c, t0, t1):
            cols = slice(t0 * P, t1 * P)
            quantize(w1_codes[c][:, cols], w1_scales[c][:, cols], w1_bf[c][:, t0:t1, :, :].rearrange("p t m j -> p (t m j)"))

        def cast_w2(u):
            nc.vector.tensor_tensor(
                out=w2_bf[u][:].rearrange("p (c i) j -> p c j i", i=2),
                in0=w2_raw[u][:].rearrange("p j (c i) -> p c j i", i=2),
                in1=hs_sign[:, entry(u), :].unsqueeze(1).unsqueeze(3).to_broadcast([P, M // 2, PACK, 2]),
                op=ALU.mult,
            )

        def quantize_w2(u):
            quantize(w2_codes[u][:], w2_scales[u][:], w2_bf[u][:].rearrange("p m j -> p (m j)"))

        def z_bank(u, t):
            g, c = units[u]
            return z_ps[g][(c * PACK + t) % Z_BANKS]

        def first_product(u, t):
            g, c = units[u]
            rows = slice(g * ROWS, (g + 1) * ROWS)
            cols = slice(t * P, (t + 1) * P)
            nc.tensor.matmul_mx(
                out=z_bank(u, t)[:],
                lhsT=w1_codes[c][rows, cols].bitcast(FP8X4),
                lhsT_scale=w1_scales[c][rows, cols],
                rhs=x_codes[rows, :].bitcast(FP8X4),
                rhs_scale=x_scales[rows, :],
                start=True,
                stop=True,
            )

        def activate(u, t):
            if PAIRED[u]:
                dst = h_out[u][:].rearrange("p (v n e) -> p v n e", v=2, e=2)[:, t // 2, :, t % 2]
            else:
                dst = h_out[u][:, t * N : (t + 1) * N]
            nc.scalar.activation(
                out=dst,
                in_=z_bank(u, t)[:],
                func=ACT.Relu,
                scale=hs_abs[:, entry(u), t : t + 1],
                bias=bias[:, entry(u), t : t + 1],
            )

        def interleave_h(copy, u, n0, n1):
            if PAIRED[u]:
                copy(
                    out=h_bf[u][:, n0:n1, :].rearrange("p n (v e) -> p n v e", e=2),
                    in_=h_out[u][:].rearrange("p (v n e) -> p n v e", v=2, e=2)[:, n0:n1, :, :],
                )
            else:
                copy(
                    out=h_bf[u][:, n0:n1, :].rearrange("p (c i) t -> p c t i", i=4),
                    in_=h_out[u][:].rearrange("p (t n) -> p t n", t=PACK)[:, :, n0:n1].rearrange("p t (c i) -> p c t i", i=4),
                )

        def quantize_h(u):
            quantize(h_codes[u][:], h_scales[u][:], h_bf[u][:].rearrange("p n t -> p (n t)"))

        def second_product(u):
            g, c = units[u]
            for t in range(M_TILES):
                cols = slice(t * P, (t + 1) * P)
                nc.tensor.matmul_mx(
                    out=y_ps[g][t][:],
                    lhsT=w2_codes[u][:, cols].bitcast(FP8X4),
                    lhsT_scale=w2_scales[u][:, cols],
                    rhs=h_codes[u][:].bitcast(FP8X4),
                    rhs_scale=h_scales[u][:],
                    start=(c == 0),
                    stop=(c == PASSES - 1),
                )

        def finish(g, t):
            nc.vector.tensor_tensor(out=res[g][t][:], in0=y_ps[g][t][:], in1=r_sb[g][:, t, :], op=ALU.add)
            nc.sync.dma_start(out=out[g, t * P : (t + 1) * P, :], in_=res[g][t][:])

        vcopy = nc.vector.tensor_copy
        scopy = nc.scalar.copy

        cast_x(vcopy, 0, X_VECTOR)
        cast_x(scopy, X_VECTOR, N)
        nc.vector.tensor_tensor(
            out=rows_dealt[:].rearrange("p e t i -> p e i t"),
            in0=rows_in[:, 0, :, :, :],
            in1=rows_in[:, 1, :, :, :],
            op=ALU.add,
        )
        quantize(x_codes[:], x_scales[:], x_bf[:].rearrange("p n j -> p (n j)"))
        nc.vector.transpose(
            out=rows_turned[:].rearrange("p e r -> p (e r)"), in_=rows_dealt[:].rearrange("p e t i -> p (e t i)")
        )
        cast_w1(scopy, 0, 0, W_FIRST_VECTOR, P // 2)
        cast_w1(vcopy, 0, 0, 0, W_FIRST_VECTOR)
        cast_w1(vcopy, 0, 1, 0, W_SECOND_VECTOR)
        cast_w1(scopy, 0, 1, W_SECOND_VECTOR, P // 2)
        nc.scalar.activation(out=hs_abs[:].rearrange("p e t -> p (e t)"), in_=rows_turned[:, :, 0], func=ACT.Abs)
        nc.scalar.activation(out=hs_sign[:].rearrange("p e t -> p (e t)"), in_=rows_turned[:, :, 0], func=ACT.Sign)
        quantize_w1(0, 0, 1)
        quantize_w1(0, 1, 2)
        nc.vector.tensor_tensor(
            out=bias[:].rearrange("p e t -> p (e t)"),
            in0=hs_abs[:].rearrange("p e t -> p (e t)"),
            in1=rows_turned[:, :, 1],
            op=ALU.mult,
        )
        quantize_w1(0, 2, 4)
        first_product(0, 0)
        first_product(0, 1)
        first_product(2, 0)
        activate(0, 0)
        first_product(0, 2)
        activate(0, 1)
        first_product(0, 3)
        first_product(2, 1)
        activate(2, 0)
        cast_w2(0)
        cast_w1(vcopy, 1, 0, 0, P // 2)
        quantize_w2(0)
        cast_w1(vcopy, 1, 1, 0, P // 2)
        quantize_w1(1, 0, 4)
        activate(0, 2)
        first_product(1, 0)
        activate(0, 3)
        first_product(1, 1)
        first_product(2, 2)
        activate(2, 1)
        activate(1, 0)
        first_product(1, 2)
        first_product(2, 3)
        activate(1, 1)
        first_product(1, 3)
        activate(2, 2)
        first_product(3, 0)
        cast_w2(1)
        interleave_h(vcopy, 0, 0, N)
        cast_w2(2)
        quantize_h(0)
        second_product(0)
        activate(1, 2)
        activate(1, 3)
        activate(2, 3)
        first_product(3, 1)
        activate(3, 0)
        first_product(3, 2)
        activate(3, 1)
        first_product(3, 3)
        activate(3, 2)
        activate(3, 3)
        quantize_w2(1)
        cast_w2(3)
        quantize_w2(2)
        interleave_h(vcopy, 1, 0, N)
        interleave_h(vcopy, 2, 0, N)
        quantize_h(1)
        second_product(1)
        quantize_h(2)
        second_product(2)
        quantize_w2(3)
        interleave_h(vcopy, 3, 0, H_LAST_VECTOR)
        interleave_h(scopy, 3, H_LAST_VECTOR, N)
        finish(0, 0)
        quantize_h(3)
        second_product(3)
        finish(0, 1)
        finish(1, 0)
        finish(1, 1)
